import numpy as np
import ml_dtypes


def mxq(x, axis, fmt="e4m3"):
    dtype, down = {"e4m3": (ml_dtypes.float8_e4m3fn, 7), "e5m2": (ml_dtypes.float8_e5m2, 14)}[fmt]
    v = np.moveaxis(np.asarray(x, np.float32).astype(ml_dtypes.bfloat16).astype(np.float64), axis, -1)
    blocks = v.reshape(v.shape[:-1] + (-1, 32))
    amax = np.abs(blocks).max(-1, keepdims=True)
    byte = np.maximum(np.where(amax > 0, np.frexp(amax)[1] - 1 + 127, 0) - down, 1)
    scale = np.exp2(byte - 127.0)
    codes = (blocks / scale).astype(np.float32).astype(dtype).astype(np.float64)
    return np.moveaxis((codes * scale).reshape(v.shape), -1, axis)


WIDE = False


def mx_kscale(k):
    if not WIDE:
        return np.ones(k)
    levels = np.array([10, -10, 5, -5, 0])
    if k % 512:
        return np.exp2(np.random.permutation(np.resize(levels, k // 32))).repeat(32)
    a = np.empty((k // 512, 16))
    for p in range(k // 512):
        a[p, :8] = np.random.permutation(np.resize(levels, 8))
        for g in range(8):
            far = levels[np.abs(levels - a[p, g]) >= 10]
            a[p, g + 8] = far[np.random.randint(len(far))]
    return np.exp2(a.ravel()).repeat(32)


def f64(x):
    return np.asarray(x).astype(np.float64)


def striped(idx):
    return np.tile(np.asarray(idx).reshape(-1, 16).T, (8, 1)).astype(np.uint16)


def unstriped(offs):
    return offs[:16].T.reshape(-1).astype(np.int64)


E2M1 = np.array([0.0, 0.5, 1.0, 1.5, 2.0, 3.0, 4.0, 6.0, -0.0, -0.5, -1.0, -1.5, -2.0, -3.0, -4.0, -6.0])


def pack_weight(w, fmt):
    k, n = w.shape
    w = f64(np.asarray(w, np.float32).astype(ml_dtypes.bfloat16)).reshape(k // 32, 32, n)
    amax = np.abs(w).max(1)
    if fmt == "e4m3":
        byte = np.frexp(amax)[1] - 1 + 127 - 7
    else:
        mant, ex = np.frexp(amax / 6.0)
        byte = np.where(mant > 0.5, ex, ex - 1) + 127
    byte = np.clip(np.where(amax > 0, byte, 1), 1, 254)
    scaled = (w * np.exp2(127.0 - byte)[:, None, :]).reshape(k, n).astype(np.float32)
    by_word = np.ascontiguousarray(scaled.reshape(k // 512, 128, 4, n).transpose(0, 1, 3, 2))
    if fmt == "e4m3":
        words = by_word.astype(ml_dtypes.float8_e4m3fn).view(np.uint8)
    else:
        c = by_word.astype(ml_dtypes.float4_e2m1fn).view(np.uint8) & 0xF
        words = (c[..., 0::2] | (c[..., 1::2] << 4)).reshape(k // 512, 128, 2 * n)
    return np.ascontiguousarray(words), np.ascontiguousarray(byte.astype(np.uint8).reshape(k // 512, 16, n))


def unpack_weight(words, scales, fmt):
    g, _, n = scales.shape
    words = np.ascontiguousarray(words).reshape(g, 128, n, -1)
    if fmt == "e4m3":
        vals = words.view(ml_dtypes.float8_e4m3fn).astype(np.float64)
    else:
        nib = np.empty((g, 128, n, 4), np.uint8)
        nib[..., 0::2] = words & 0xF
        nib[..., 1::2] = words >> 4
        vals = E2M1[nib]
    vals = vals * np.repeat(np.exp2(scales.astype(np.float64) - 127.0), 8, axis=1)[..., None]
    return vals.transpose(0, 1, 3, 2).reshape(g * 512, n)


K, R, F, T, J, G = 512, 128, 512, 2048, 512, 64


def setup_inputs():
    n = np.random.standard_normal
    idx = np.random.permutation(T)[:J]
    fk = mx_kscale(K)
    ff = mx_kscale(F)
    fj = mx_kscale(J)
    tj = np.ones(T)
    tj[idx] = fj
    tabp = pack_weight(n((K, T)) / fk[:, None], "e4m3")
    return {
        "tab_words": tabp[0],
        "tab_scales": tabp[1],
        "w1": (n((K, R)) * 1.5 / np.sqrt(K) * fk[:, None]).astype(np.float32),
        "w2": (n((K, R)) * 0.7 / np.sqrt(K) * fk[:, None]).astype(np.float32),
        "wo": (n((F, R)) * 1 / np.sqrt(F) * ff[:, None]).astype(np.float32),
        "dy": (n((F, G)) / ff[:, None]).astype(np.float32),
        "js": (np.random.uniform(0.5, 2.0, (1, J)) * fj).astype(np.float32),
        "xrows": (n((K, T)) / tj).astype(np.float32),
        "old": (n((K, R)) * 4.0).astype(np.float32),
        "offs": striped(idx),
    }


def reference(tab_words, tab_scales, w1, w2, wo, dy, js, xrows, old, offs):
    idx = unstriped(offs)
    tabu = unpack_weight(tab_words, tab_scales, "e4m3")
    w1q = mxq(f64(w1), 0, "e4m3")
    tabidxg = tabu[:, idx]
    a = w1q.T @ tabidxg
    w2q = mxq(f64(w2), 0, "e4m3")
    b = w2q.T @ tabidxg
    p = np.exp(b)
    z = p.reshape(R, G, J // G).sum(axis=2)
    n1 = (p * a).reshape(R, G, J // G).sum(axis=2)
    u1 = np.tanh(n1 / z)
    woq = mxq(f64(wo), 0, "e4m3")
    dyq = mxq(f64(dy), 0, "e4m3")
    c0 = woq.T @ dyq
    dn1 = c0 * (1.0 - np.square(u1)) / z
    r1 = np.repeat(dn1, J // G, axis=1)
    dz = c0 * (1.0 - np.square(u1)) * n1 / np.square(z) * (-1.0)
    r2 = np.repeat(dz, J // G, axis=1)
    dp = r1 * a + r2
    db = dp * p
    gs = db * f64(js)
    gt1 = gs.T
    xt = f64(xrows)[:, idx].T
    xtq = mxq(xt, 0, "e4m3")
    gt1q = mxq(gt1, 0, "e4m3")
    gw = xtq.T @ gt1q
    y = gw + f64(old)
    return y

@@ -1,0 +1,221 @@
+from contextlib import ExitStack
+
+import concourse.mybir as mybir
+from concourse.masks import make_identity
+
+K, R, F, T, J, G = 512, 128, 512, 2048, 512, 64
+FLOPS = 2 * (2 * K * R * J + F * R * G + J * K * R)
+
+F32 = mybir.dt.float32
+BF16 = mybir.dt.bfloat16
+I32 = mybir.dt.int32
+U32 = mybir.dt.uint32
+U16 = mybir.dt.uint16
+U8 = mybir.dt.uint8
+FP8X4 = mybir.dt.float8_e4m3fn_x4
+ALU = mybir.AluOpType
+ACT = mybir.ActivationFunctionType
+AXIS = mybir.AxisListType
+
+P = 128
+PACK = 4
+
+
+def tile_attend_cgatepool_b_w_kernel(tc, tab_words, tab_scales, w1, w2, wo, dy, js, xrows, old, offs, out):
+    nc = tc.nc
+    with ExitStack() as ctx:
+        sb = ctx.enter_context(tc.tile_pool(name="sb", bufs=1))
+        ps = ctx.enter_context(tc.psum_pool(name="ps", bufs=1))
+
+        offsets = sb.tile([P, J // 16], U16, name="offsets")
+        tab_bytes = sb.tile([P, T], U8, name="tab_bytes", tag="tab_bytes", align_bytes=64)
+        tab_w = sb.tile([P, T], I32, name="tab_w", align_bytes=64)
+        nc.gpsimd.memset(tab_bytes[:].bitcast(I32), 0)
+        nc.sync.dma_start(offsets[:], offs)
+        for q in range(4):
+            nc.scalar.dma_start(
+                out=tab_bytes[32 * q : 32 * q + 4, :].bitcast(I32),
+                in_=tab_scales[0, 4 * q : 4 * q + 4, :].bitcast(I32),
+            )
+        nc.sync.dma_start(out=tab_w[:], in_=tab_words[0].rearrange("p n t -> p (n t)").bitcast(I32))
+
+        def load_rows(name, src, width):
+            raw = sb.tile([P, PACK, width], F32, name=name + "_raw")
+            nc.sync.dma_start(out=raw[:], in_=src.rearrange("(p t) c -> p t c", t=PACK))
+            return raw
+
+        w2_raw = load_rows("w2", w2, R)
+        w1_raw = load_rows("w1", w1, R)
+        x_rows = xrows.rearrange("(p m) n -> p m n", m=PACK)
+
+        def load_x(m):
+            xm = sb.tile([P, T], F32, name="x_all%d" % m, tag="x_all%d" % m, align_bytes=64)
+            nc.sync.dma_start(out=xm[:], in_=x_rows[:, m, :])
+            return xm
+
+        wo_raw = load_rows("wo", wo, R)
+        dy_raw = load_rows("dy", dy, G)
+        js_col = sb.tile([P, PACK], F32, name="js_col")
+        nc.sync.dma_start(out=js_col[:], in_=js.rearrange("o (p t) -> p (o t)", t=PACK))
+        x_all = [load_x(m) for m in range(PACK)]
+        old_sb = load_rows("old", old, R)
+
+        ident = sb.tile([P, P], F32, name="ident")
+        make_identity(nc, ident[:])
+
+        def quantize(name, grouped, width):
+            codes = sb.tile([P, width], U32, name=name + "_codes", align_bytes=64)
+            scales = sb.tile([P, width], U8, name=name + "_scales", align_bytes=64)
+            nc.vector.quantize_mx(
+                out=codes[:].bitcast(FP8X4), scales=scales[:], in_=grouped[:].rearrange("p c t -> p (c t)")
+            )
+            return codes, scales
+
+        def interleave(name, raw, width):
+            grouped = sb.tile([P, width, PACK], BF16, name=name + "_grouped", align_bytes=64)
+            nc.scalar.copy(out=grouped[:], in_=raw[:].rearrange("p t c -> p c t"))
+            return grouped
+
+        def product(acc, lhs, rhs):
+            nc.tensor.matmul_mx(
+                out=acc,
+                lhsT=lhs[0][:].bitcast(FP8X4),
+                lhsT_scale=lhs[1][:],
+                rhs=rhs[0][:].bitcast(FP8X4),
+                rhs_scale=rhs[1][:],
+                start=True,
+                stop=True,
+            )
+
+        listed_bytes = sb.tile([P, J], U8, name="listed_bytes", align_bytes=64)
+        nc.vector.tensor_copy(listed_bytes[:], tab_bytes[:].indirect(offsets[:]))
+        listed_w = sb.tile([P, J], U32, name="listed_w", tag="tab_bytes", align_bytes=64)
+        nc.vector.tensor_copy(listed_w[:], tab_w[:].bitcast(U32).indirect(offsets[:]))
+        listed = (listed_w, listed_bytes)
+
+        def listed_x(m, tag):
+            picked = sb.tile([P, J], BF16, name="x_picked%d" % m, tag=tag, align_bytes=64)
+            nc.vector.tensor_copy(picked[:], x_all[m][:].indirect(offsets[:]))
+            pairs = picked[:].bitcast(F32)
+            turned = ps.tile([P, 2, P], F32, name="x_turned", tag="x_turned", bufs=2)
+            for u in range(2):
+                nc.tensor.transpose(turned[:, u, :], pairs[:, u : J // 2 : 2], ident[:])
+            grouped = sb.tile([P, P, PACK], BF16, name="x_grouped%d" % m, align_bytes=64)
+            nc.scalar.copy(
+                out=grouped[:].rearrange("p c t -> p (c t)").bitcast(F32).rearrange("p (c u) -> p c u", u=2),
+                in_=turned[:].rearrange("p u c -> p c u"),
+            )
+            return grouped
+
+        w2_q = quantize("w2", interleave("w2", w2_raw, R), R)
+        w1_q = quantize("w1", interleave("w1", w1_raw, R), R)
+        b_ps = ps.tile([P, J], F32, name="b_ps", tag="bank_b")
+        a_ps = ps.tile([P, J], F32, name="a_ps", tag="bank_a")
+        product(b_ps[:], w2_q, listed)
+        product(a_ps[:], w1_q, listed)
+
+        wo_q = quantize("wo", interleave("wo", wo_raw, R), R)
+        dy_q = quantize("dy", interleave("dy", dy_raw, G), G)
+        c0_ps = ps.tile([P, G], F32, name="c0_ps")
+        product(c0_ps[:], wo_q, dy_q)
+
+        neg_max = sb.tile([P, G], F32, name="neg_max", tag="neg_max", align_bytes=64)
+        nc.vector.tensor_reduce(
+            out=neg_max[:], in_=b_ps[:].rearrange("p (g i) -> p g i", i=8), axis=AXIS.X, op=ALU.max, negate=True
+        )
+        shifted = sb.tile([P, PACK, 2, G], F32, name="shifted", tag="shifted", align_bytes=64)
+        nc.vector.tensor_tensor(
+            out=shifted[:],
+            in0=b_ps[:].rearrange("p (g h t) -> p t h g", h=2, t=PACK),
+            in1=neg_max[:].unsqueeze(1).unsqueeze(1).to_broadcast([P, PACK, 2, G]),
+            op=ALU.add,
+        )
+        terms = sb.tile([P, PACK, 2, 2, G], F32, name="terms")
+        nc.scalar.activation(out=terms[:, :, :, 1, :], in_=shifted[:], func=ACT.Exp)
+        x_grouped = [listed_x(0, "neg_max")]
+        nc.vector.tensor_tensor(
+            out=terms[:, :, :, 0, :],
+            in0=a_ps[:].rearrange("p (g h t) -> p t h g", h=2, t=PACK),
+            in1=terms[:, :, :, 1, :],
+            op=ALU.mult,
+        )
+        sums_t = ps.tile([P, R], F32, name="sums_t", tag="bank_b")
+        by_slot = terms[:].rearrange("p t h s g -> p (t h) (s g)")
+        for i in range(8):
+            nc.tensor.matmul(
+                out=sums_t[:], lhsT=by_slot[:, i, :], rhs=ident[:], is_transpose=True, start=(i == 0), stop=(i == 7)
+            )
+        sums_t_sb = sb.tile([P, R], F32, name="sums_t_sb")
+        nc.scalar.copy(out=sums_t_sb[:], in_=sums_t[:])
+        sums = ps.tile([P, 2, G], F32, name="sums")
+        nc.tensor.transpose(sums[:].rearrange("p s g -> p (s g)"), sums_t_sb[:], ident[:])
+        x_grouped.append(listed_x(1, "shifted"))
+        x_q = [quantize("x0", x_grouped[0], P)]
+
+
+        inv_z = sb.tile([P, G], F32, name="inv_z", tag="x_all1", align_bytes=64)
+        nc.vector.reciprocal(out=inv_z[:], in_=sums[:, 1, :])
+        mean = sb.tile([P, G], F32, name="mean")
+        nc.vector.tensor_tensor(out=mean[:], in0=sums[:, 0, :], in1=inv_z[:], op=ALU.mult)
+        u1 = sb.tile([P, G], F32, name="u1")
+        nc.scalar.activation(out=u1[:], in_=mean[:], func=ACT.Tanh)
+        u1_sq = sb.tile([P, G], F32, name="u1_sq")
+        nc.scalar.activation(out=u1_sq[:], in_=u1[:], func=ACT.Square)
+        upstream = sb.tile([P, 2, G], F32, name="upstream")
+        nc.vector.tensor_tensor(out=upstream[:, 0, :], in0=c0_ps[:], in1=inv_z[:], op=ALU.mult)
+        x_q.append(quantize("x1", x_grouped[1], P))
+        nc.vector.scalar_tensor_tensor(
+            out=upstream[:, 1, :], in0=upstream[:, 0, :], scalar=-1.0, in1=mean[:], op0=ALU.mult, op1=ALU.mult
+        )
+        x_grouped.append(listed_x(2, "picked2"))
+        neg_coef = sb.tile([P, 2, G], F32, name="neg_coef", tag="x_all2", align_bytes=64)
+        nc.vector.scalar_tensor_tensor(
+            out=neg_coef[:],
+            in0=u1_sq[:].unsqueeze(1).to_broadcast([P, 2, G]),
+            scalar=1.0,
+            in1=upstream[:],
+            op0=ALU.subtract,
+            op1=ALU.mult,
+        )
+        weighted = sb.tile([P, PACK, 2 * G, 2], F32, name="weighted")
+        nc.vector.tensor_tensor(
+            out=weighted[:],
+            in0=terms[:].rearrange("p t h s g -> p t (s g) h"),
+            in1=neg_coef[:].rearrange("p s g -> p (s g)").unsqueeze(1).unsqueeze(3).to_broadcast([P, PACK, 2 * G, 2]),
+            op=ALU.mult,
+        )
+        halves = weighted[:].rearrange("p t (s g) h -> p t s (g h)", s=2)
+        neg_db_t = ps.tile([P, PACK, P], F32, name="neg_db_t", tag="bank_a")
+        for t in range(PACK):
+            for s in range(2):
+                nc.tensor.matmul(
+                    out=neg_db_t[:, t, :],
+                    lhsT=halves[:, t, s, :],
+                    rhs=ident[:],
+                    is_transpose=True,
+                    start=(s == 0),
+                    stop=(s == 1),
+                )
+        x_grouped.append(listed_x(3, "picked3"))
+        x_q.append(quantize("x2", x_grouped[2], P))
+        gt_grouped = sb.tile([P, R, PACK], BF16, name="gt_grouped", tag="x_all3", align_bytes=64)
+        nc.vector.scalar_tensor_tensor(
+            out=gt_grouped[:],
+            in0=neg_db_t[:].rearrange("p t r -> p r t"),
+            scalar=-1.0,
+            in1=js_col[:].unsqueeze(1).to_broadcast([P, R, PACK]),
+            op0=ALU.mult,
+            op1=ALU.mult,
+        )
+        gt_q = quantize("gt", gt_grouped, R)
+        x_q.append(quantize("x3", x_grouped[3], P))
+
+        out_rows = out.rearrange("(p m) r -> p m r", m=PACK)
+        result = sb.tile([P, PACK, R], F32, name="result")
+        for half in range(2):
+            tiles = slice(2 * half, 2 * half + 2)
+            gw_ps = ps.tile([P, 2, R], F32, name="gw_ps%d" % half)
+            for m in range(2):
+                product(gw_ps[:, m, :], x_q[2 * half + m], gt_q)
+            nc.vector.tensor_tensor(out=result[:, tiles, :], in0=gw_ps[:], in1=old_sb[:, tiles, :], op=ALU.add)
+            nc.sync.dma_start(out=out_rows[:, tiles, :], in_=result[:, tiles, :])

@@ -29,7 +29,7 @@ def tile_attend_cgatepool_b_w_kernel(tc, tab_words, tab_scales, w1, w2, wo, dy, 
 
         offsets = sb.tile([P, J // 16], U16, name="offsets")
         tab_bytes = sb.tile([P, T], U8, name="tab_bytes", tag="tab_bytes", align_bytes=64)
-        tab_w = sb.tile([P, T], I32, name="tab_w", align_bytes=64)
+        tab_w = sb.tile([P, T], I32, name="tab_w", tag="tab_w", align_bytes=64)
         nc.gpsimd.memset(tab_bytes[:].bitcast(I32), 0)
         nc.sync.dma_start(offsets[:], offs)
         for q in range(4):
@@ -53,169 +53,208 @@ def tile_attend_cgatepool_b_w_kernel(tc, tab_words, tab_scales, w1, w2, wo, dy, 
             nc.sync.dma_start(out=xm[:], in_=x_rows[:, m, :])
             return xm
 
+        x_rows = xrows.rearrange("(p m) n -> p m n", m=PACK)
+
+        def load_x(m):
+            xm = sb.tile([P, T], F32, name="x_all%d" % m, tag="x_all%d" % m, align_bytes=64)
+            nc.sync.dma_start(out=xm[:], in_=x_rows[:, m, :])
+            return xm
+
         wo_raw = load_rows("wo", wo, R)
         dy_raw = load_rows("dy", dy, G)
         js_col = sb.tile([P, PACK], F32, name="js_col")
         nc.sync.dma_start(out=js_col[:], in_=js.rearrange("o (p t) -> p (o t)", t=PACK))
-        x_all = [load_x(m) for m in range(PACK)]
+        x_all = {m: load_x(m) for m in (0, 2, 1, 3)}
         old_sb = load_rows("old", old, R)
 
         ident = sb.tile([P, P], F32, name="ident")
         make_identity(nc, ident[:])
 
-        def quantize(name, grouped, width):
-            codes = sb.tile([P, width], U32, name=name + "_codes", align_bytes=64)
+        def quantize(name, grouped, width, codes=None):
+            if codes is None:
+                codes = sb.tile([P, width], U32, name=name + "_codes", align_bytes=64)[:]
             scales = sb.tile([P, width], U8, name=name + "_scales", align_bytes=64)
             nc.vector.quantize_mx(
-                out=codes[:].bitcast(FP8X4), scales=scales[:], in_=grouped[:].rearrange("p c t -> p (c t)")
+                out=codes.bitcast(FP8X4), scales=scales[:], in_=grouped.rearrange("p c t -> p (c t)")
             )
-            return codes, scales
+            return codes, scales[:]
 
-        def interleave(name, raw, width):
-            grouped = sb.tile([P, width, PACK], BF16, name=name + "_grouped", align_bytes=64)
-            nc.scalar.copy(out=grouped[:], in_=raw[:].rearrange("p t c -> p c t"))
+        def interleave(copy, grouped, raw):
+            copy(out=grouped, in_=raw[:].rearrange("p t c -> p c t"))
             return grouped
 
         def product(acc, lhs, rhs):
             nc.tensor.matmul_mx(
                 out=acc,
-                lhsT=lhs[0][:].bitcast(FP8X4),
-                lhsT_scale=lhs[1][:],
-                rhs=rhs[0][:].bitcast(FP8X4),
-                rhs_scale=rhs[1][:],
+                lhsT=lhs[0].bitcast(FP8X4),
+                lhsT_scale=lhs[1],
+                rhs=rhs[0].bitcast(FP8X4),
+                rhs_scale=rhs[1],
                 start=True,
                 stop=True,
             )
 
-        listed_bytes = sb.tile([P, J], U8, name="listed_bytes", align_bytes=64)
-        nc.vector.tensor_copy(listed_bytes[:], tab_bytes[:].indirect(offsets[:]))
-        listed_w = sb.tile([P, J], U32, name="listed_w", tag="tab_bytes", align_bytes=64)
-        nc.vector.tensor_copy(listed_w[:], tab_w[:].bitcast(U32).indirect(offsets[:]))
-        listed = (listed_w, listed_bytes)
-
-        def listed_x(m, tag):
-            picked = sb.tile([P, J], BF16, name="x_picked%d" % m, tag=tag, align_bytes=64)
-            nc.vector.tensor_copy(picked[:], x_all[m][:].indirect(offsets[:]))
-            pairs = picked[:].bitcast(F32)
-            turned = ps.tile([P, 2, P], F32, name="x_turned", tag="x_turned", bufs=2)
+        def turn(name, values, bank):
+            pairs = values[:].bitcast(F32)
+            turned = ps.tile([P, 2, P], F32, name=name + "_turned", tag=bank)
             for u in range(2):
                 nc.tensor.transpose(turned[:, u, :], pairs[:, u : J // 2 : 2], ident[:])
-            grouped = sb.tile([P, P, PACK], BF16, name="x_grouped%d" % m, align_bytes=64)
+            return turned
+
+        def lay_out(grouped, turned):
             nc.scalar.copy(
-                out=grouped[:].rearrange("p c t -> p (c t)").bitcast(F32).rearrange("p (c u) -> p c u", u=2),
+                out=grouped.rearrange("p c t -> p (c t)").bitcast(F32).rearrange("p (c u) -> p c u", u=2),
                 in_=turned[:].rearrange("p u c -> p c u"),
             )
-            return grouped
 
-        w2_q = quantize("w2", interleave("w2", w2_raw, R), R)
-        w1_q = quantize("w1", interleave("w1", w1_raw, R), R)
-        b_ps = ps.tile([P, J], F32, name="b_ps", tag="bank_b")
+        def pick_on_vector(m, tag):
+            picked = sb.tile([P, J], BF16, name="x_picked%d" % m, tag=tag, align_bytes=64)
+            nc.vector.tensor_copy(picked[:], x_all[m][:].indirect(offsets[:]))
+            return picked
+
+        def pick_on_scalar(m):
+            rounded = sb.tile([P, T], BF16, name="x_rounded%d" % m, tag="shifted", align_bytes=64)
+            nc.scalar.activation(out=rounded[:], in_=x_all[m][:], func=ACT.Copy)
+            picked = sb.tile([P, J], BF16, name="x_picked%d" % m, align_bytes=64)
+            nc.scalar.activation(picked[:], rounded[:].indirect(offsets[:]), ACT.Copy)
+            return picked
+
+        def codes_tile(name, width, tag):
+            return sb.tile([P, width], U32, name=name, tag=tag, align_bytes=64)[:]
+
+        HJ, HG = J // 2, G // 2
+        listed_w = sb.tile([P, J], U32, name="listed_w", align_bytes=64)
+        nc.vector.tensor_copy(listed_w[:], tab_w[:].bitcast(U32).indirect(offsets[:]))
+        w2_grouped = sb.tile([P, R, PACK], BF16, name="w2_grouped", tag="w2_grouped", align_bytes=64)
+        w1_grouped = sb.tile([P, R, PACK], BF16, name="w1_grouped", align_bytes=64)
+        interleave(nc.scalar.copy, w2_grouped[:], w2_raw)
+        interleave(nc.scalar.copy, w1_grouped[:], w1_raw)
+        wo_grouped = sb.tile([P, R, PACK], BF16, name="wo_grouped", align_bytes=64)
+        dy_grouped = sb.tile([P, G, PACK], BF16, name="dy_grouped", align_bytes=64)
+        interleave(nc.scalar.copy, wo_grouped[:], wo_raw)
+        interleave(nc.scalar.copy, dy_grouped[:], dy_raw)
+        b_ps, listed = [], []
+        for c in range(2):
+            cols = slice(c * HJ, (c + 1) * HJ)
+            listed_bytes = sb.tile(
+                [P, HJ], U8, name="listed_bytes%d" % c, tag=("listed_bytes", "w2_grouped")[c], align_bytes=64
+            )
+            nc.vector.tensor_copy(
+                listed_bytes[:], tab_bytes[:].indirect(offsets[:, c * HJ // 16 : (c + 1) * HJ // 16])
+            )
+            listed.append((listed_w[:, cols], listed_bytes[:]))
+            if c == 0:
+                w2_q = quantize("w2", w2_grouped[:], R)
+            b_ps.append(ps.tile([P, HJ], F32, name="b_ps%d" % c, tag="bank_b%d" % c))
+            product(b_ps[c][:], w2_q, listed[c])
+        w1_q = quantize("w1", w1_grouped[:], R)
         a_ps = ps.tile([P, J], F32, name="a_ps", tag="bank_a")
-        product(b_ps[:], w2_q, listed)
-        product(a_ps[:], w1_q, listed)
+        for c in range(2):
+            product(a_ps[:, c * HJ : (c + 1) * HJ], w1_q, listed[c])
 
-        wo_q = quantize("wo", interleave("wo", wo_raw, R), R)
-        dy_q = quantize("dy", interleave("dy", dy_raw, G), G)
-        c0_ps = ps.tile([P, G], F32, name="c0_ps")
-        product(c0_ps[:], wo_q, dy_q)
+        def by_group(ap):
+            return ap.rearrange("p (g i) -> p g i", i=8)
+
+        def over_group(ap, groups):
+            return ap.unsqueeze(2).to_broadcast([P, groups, 8])
 
         neg_max = sb.tile([P, G], F32, name="neg_max", tag="neg_max", align_bytes=64)
-        nc.vector.tensor_reduce(
-            out=neg_max[:], in_=b_ps[:].rearrange("p (g i) -> p g i", i=8), axis=AXIS.X, op=ALU.max, negate=True
-        )
-        shifted = sb.tile([P, PACK, 2, G], F32, name="shifted", tag="shifted", align_bytes=64)
-        nc.vector.tensor_tensor(
-            out=shifted[:],
-            in0=b_ps[:].rearrange("p (g h t) -> p t h g", h=2, t=PACK),
-            in1=neg_max[:].unsqueeze(1).unsqueeze(1).to_broadcast([P, PACK, 2, G]),
-            op=ALU.add,
-        )
-        terms = sb.tile([P, PACK, 2, 2, G], F32, name="terms")
-        nc.scalar.activation(out=terms[:, :, :, 1, :], in_=shifted[:], func=ACT.Exp)
-        x_grouped = [listed_x(0, "neg_max")]
-        nc.vector.tensor_tensor(
-            out=terms[:, :, :, 0, :],
-            in0=a_ps[:].rearrange("p (g h t) -> p t h g", h=2, t=PACK),
-            in1=terms[:, :, :, 1, :],
-            op=ALU.mult,
-        )
-        sums_t = ps.tile([P, R], F32, name="sums_t", tag="bank_b")
-        by_slot = terms[:].rearrange("p t h s g -> p (t h) (s g)")
-        for i in range(8):
-            nc.tensor.matmul(
-                out=sums_t[:], lhsT=by_slot[:, i, :], rhs=ident[:], is_transpose=True, start=(i == 0), stop=(i == 7)
+        shifted = sb.tile([P, J], F32, name="shifted", tag="shifted", align_bytes=64)
+        p = sb.tile([P, J], F32, name="p")
+        for c in range(2):
+            nc.vector.tensor_reduce(
+                out=neg_max[:, c * HG : (c + 1) * HG], in_=by_group(b_ps[c][:]), axis=AXIS.X, op=ALU.max, negate=True
             )
-        sums_t_sb = sb.tile([P, R], F32, name="sums_t_sb")
-        nc.scalar.copy(out=sums_t_sb[:], in_=sums_t[:])
-        sums = ps.tile([P, 2, G], F32, name="sums")
-        nc.tensor.transpose(sums[:].rearrange("p s g -> p (s g)"), sums_t_sb[:], ident[:])
-        x_grouped.append(listed_x(1, "shifted"))
-        x_q = [quantize("x0", x_grouped[0], P)]
+        for c in range(2):
+            cols = slice(c * HJ, (c + 1) * HJ)
+            nc.vector.tensor_tensor(
+                out=by_group(shifted[:, cols]),
+                in0=by_group(b_ps[c][:]),
+                in1=over_group(neg_max[:, c * HG : (c + 1) * HG], HG),
+                op=ALU.add,
+            )
+            nc.scalar.activation(out=p[:, cols], in_=shifted[:, cols], func=ACT.Exp)
+        c0_codes = codes_tile("c0_codes", R + G, "neg_max")
+        wo_q = quantize("wo", wo_grouped[:], R, c0_codes[:, 0:R])
+        dy_q = quantize("dy", dy_grouped[:], G, c0_codes[:, R : R + G])
+        c0_ps = ps.tile([P, G], F32, name="c0_ps", tag="bank_c0")
+        product(c0_ps[:], wo_q, dy_q)
+        js_rows = ps.tile([P, PACK, P], F32, name="js_rows", tag="bank_b0")
+        for t in range(PACK):
+            nc.tensor.transpose(js_rows[:, t, :], js_col[:, t : t + 1].to_broadcast([P, P]), ident[:])
+        x0_turned = turn("x0", pick_on_scalar(0), "bank_x0")
 
+        def group_sums(name, values):
+            total = sb.tile([P, G], F32, name=name)
+            nc.vector.tensor_reduce(out=total[:], in_=by_group(values[:]), axis=AXIS.X, op=ALU.add)
+            return total
 
-        inv_z = sb.tile([P, G], F32, name="inv_z", tag="x_all1", align_bytes=64)
-        nc.vector.reciprocal(out=inv_z[:], in_=sums[:, 1, :])
-        mean = sb.tile([P, G], F32, name="mean")
-        nc.vector.tensor_tensor(out=mean[:], in0=sums[:, 0, :], in1=inv_z[:], op=ALU.mult)
-        u1 = sb.tile([P, G], F32, name="u1")
-        nc.scalar.activation(out=u1[:], in_=mean[:], func=ACT.Tanh)
+        z = group_sums("z", p)
+        pa = sb.tile([P, J], F32, name="pa")
+        nc.vector.tensor_tensor(out=pa[:], in0=a_ps[:], in1=p[:], op=ALU.mult)
+        inv_z = sb.tile([P, G], F32, name="inv_z")
+        nc.vector.reciprocal(out=inv_z[:], in_=z[:])
+        n1 = group_sums("n1", pa)
+        c0_by_z = sb.tile([P, G], F32, name="c0_by_z")
+        nc.vector.tensor_tensor(out=c0_by_z[:], in0=c0_ps[:], in1=inv_z[:], op=ALU.mult)
+        neg_mean = sb.tile([P, G], F32, name="neg_mean")
+        nc.vector.scalar_tensor_tensor(
+            out=neg_mean[:], in0=n1[:], scalar=-1.0, in1=inv_z[:], op0=ALU.mult, op1=ALU.mult
+        )
+        u1 = sb.tile([P, G], F32, name="u1", tag="shifted", align_bytes=64)
+        nc.scalar.activation(out=u1[:], in_=neg_mean[:], func=ACT.Tanh)
         u1_sq = sb.tile([P, G], F32, name="u1_sq")
         nc.scalar.activation(out=u1_sq[:], in_=u1[:], func=ACT.Square)
-        upstream = sb.tile([P, 2, G], F32, name="upstream")
-        nc.vector.tensor_tensor(out=upstream[:, 0, :], in0=c0_ps[:], in1=inv_z[:], op=ALU.mult)
-        x_q.append(quantize("x1", x_grouped[1], P))
+        x2_picked = pick_on_scalar(2)
+
+        p_js = sb.tile([P, J], F32, name="p_js")
         nc.vector.scalar_tensor_tensor(
-            out=upstream[:, 1, :], in0=upstream[:, 0, :], scalar=-1.0, in1=mean[:], op0=ALU.mult, op1=ALU.mult
-        )
-        x_grouped.append(listed_x(2, "picked2"))
-        neg_coef = sb.tile([P, 2, G], F32, name="neg_coef", tag="x_all2", align_bytes=64)
-        nc.vector.scalar_tensor_tensor(
-            out=neg_coef[:],
-            in0=u1_sq[:].unsqueeze(1).to_broadcast([P, 2, G]),
-            scalar=1.0,
-            in1=upstream[:],
-            op0=ALU.subtract,
-            op1=ALU.mult,
-        )
-        weighted = sb.tile([P, PACK, 2 * G, 2], F32, name="weighted")
-        nc.vector.tensor_tensor(
-            out=weighted[:],
-            in0=terms[:].rearrange("p t h s g -> p t (s g) h"),
-            in1=neg_coef[:].rearrange("p s g -> p (s g)").unsqueeze(1).unsqueeze(3).to_broadcast([P, PACK, 2 * G, 2]),
-            op=ALU.mult,
-        )
-        halves = weighted[:].rearrange("p t (s g) h -> p t s (g h)", s=2)
-        neg_db_t = ps.tile([P, PACK, P], F32, name="neg_db_t", tag="bank_a")
-        for t in range(PACK):
-            for s in range(2):
-                nc.tensor.matmul(
-                    out=neg_db_t[:, t, :],
-                    lhsT=halves[:, t, s, :],
-                    rhs=ident[:],
-                    is_transpose=True,
-                    start=(s == 0),
-                    stop=(s == 1),
-                )
-        x_grouped.append(listed_x(3, "picked3"))
-        x_q.append(quantize("x2", x_grouped[2], P))
-        gt_grouped = sb.tile([P, R, PACK], BF16, name="gt_grouped", tag="x_all3", align_bytes=64)
-        nc.vector.scalar_tensor_tensor(
-            out=gt_grouped[:],
-            in0=neg_db_t[:].rearrange("p t r -> p r t"),
+            out=p_js[:].rearrange("p (q t) -> p q t", t=PACK),
+            in0=js_rows[:].rearrange("p t q -> p q t"),
             scalar=-1.0,
-            in1=js_col[:].unsqueeze(1).to_broadcast([P, R, PACK]),
+            in1=p[:].rearrange("p (q t) -> p q t", t=PACK),
             op0=ALU.mult,
             op1=ALU.mult,
         )
-        gt_q = quantize("gt", gt_grouped, R)
-        x_q.append(quantize("x3", x_grouped[3], P))
+        centred = sb.tile([P, J], F32, name="centred")
+        nc.vector.tensor_tensor(
+            out=by_group(centred[:]), in0=by_group(a_ps[:]), in1=over_group(neg_mean[:], G), op=ALU.add
+        )
+        neg_dn1 = sb.tile([P, G], F32, name="neg_dn1", tag="neg_dn1", align_bytes=64)
+        nc.vector.scalar_tensor_tensor(
+            out=neg_dn1[:], in0=u1_sq[:], scalar=1.0, in1=c0_by_z[:], op0=ALU.subtract, op1=ALU.mult
+        )
+        spread = sb.tile([P, J], F32, name="spread")
+        nc.vector.tensor_tensor(out=spread[:], in0=centred[:], in1=p_js[:], op=ALU.mult)
+        gs = sb.tile([P, J], BF16, name="gs", align_bytes=64)
+        nc.vector.tensor_tensor(
+            out=by_group(gs[:]), in0=by_group(spread[:]), in1=over_group(neg_dn1[:], G), op=ALU.mult
+        )
+        gt_grouped = sb.tile([P, R, PACK], BF16, name="gt_grouped", align_bytes=64)
+        lay_out(gt_grouped[:], turn("gs", gs, "bank_b1"))
+
+        x1_turned = turn("x1", pick_on_vector(1, "neg_dn1"), "bank_a")
+        x01_grouped = sb.tile([P, 2 * P, PACK], BF16, name="x01_grouped", tag="shifted", align_bytes=64)
+        lay_out(x01_grouped[:, 0:P, :], x0_turned)
+        lay_out(x01_grouped[:, P : 2 * P, :], x1_turned)
+        x2_grouped = sb.tile([P, P, PACK], BF16, name="x2_grouped", align_bytes=64)
+        x3_grouped = sb.tile([P, P, PACK], BF16, name="x3_grouped", tag="x3_grouped", align_bytes=64)
+        lay_out(x2_grouped[:], turn("x2", x2_picked, "bank_c0"))
+        lay_out(x3_grouped[:], turn("x3", pick_on_vector(3, "x_picked3"), "bank_b0"))
+
+        last_codes = codes_tile("last_codes", R + 3 * P, "x_all3")
+        gt_q = quantize("gt", gt_grouped[:], R, last_codes[:, 0:R])
+        x01_q = quantize("x01", x01_grouped[:], 2 * P, last_codes[:, R : R + 2 * P])
+        x2_q = quantize("x2", x2_grouped[:], P, last_codes[:, R + 2 * P : R + 3 * P])
+        x3_q = quantize("x3", x3_grouped[:], P)
+        x_q = [[plane[:, 0:P] for plane in x01_q], [plane[:, P : 2 * P] for plane in x01_q], x2_q, x3_q]
 
         out_rows = out.rearrange("(p m) r -> p m r", m=PACK)
-        result = sb.tile([P, PACK, R], F32, name="result")
-        for half in range(2):
-            tiles = slice(2 * half, 2 * half + 2)
-            gw_ps = ps.tile([P, 2, R], F32, name="gw_ps%d" % half)
+        result = sb.tile([P, PACK, R], F32, name="result", tag="x3_grouped", align_bytes=64)
+        for c in range(2):
+            tiles = slice(2 * c, 2 * c + 2)
+            gw_ps = ps.tile([P, 2, R], F32, name="gw_ps%d" % c)
             for m in range(2):
-                product(gw_ps[:, m, :], x_q[2 * half + m], gt_q)
+                product(gw_ps[:, m, :], x_q[2 * c + m], gt_q)
             nc.vector.tensor_tensor(out=result[:, tiles, :], in0=gw_ps[:], in1=old_sb[:, tiles, :], op=ALU.add)
             nc.sync.dma_start(out=out_rows[:, tiles, :], in_=result[:, tiles, :])

from contextlib import ExitStack

import concourse.mybir as mybir
from concourse.masks import make_identity

K, R, F, T, J, G = 512, 128, 512, 2048, 512, 64
FLOPS = 2 * (2 * K * R * J + F * R * G + J * K * R)

F32 = mybir.dt.float32
BF16 = mybir.dt.bfloat16
I32 = mybir.dt.int32
U32 = mybir.dt.uint32
U16 = mybir.dt.uint16
U8 = mybir.dt.uint8
FP8X4 = mybir.dt.float8_e4m3fn_x4
ALU = mybir.AluOpType
ACT = mybir.ActivationFunctionType
AXIS = mybir.AxisListType

P = 128
PACK = 4


def tile_attend_cgatepool_b_w_kernel(tc, tab_words, tab_scales, w1, w2, wo, dy, js, xrows, old, offs, out):
    nc = tc.nc
    with ExitStack() as ctx:
        sb = ctx.enter_context(tc.tile_pool(name="sb", bufs=1))
        ps = ctx.enter_context(tc.psum_pool(name="ps", bufs=1))

        offsets = sb.tile([P, J // 16], U16, name="offsets")
        tab_bytes = sb.tile([P, T], U8, name="tab_bytes", tag="tab_bytes", align_bytes=64)
        tab_w = sb.tile([P, T], I32, name="tab_w", tag="tab_w", align_bytes=64)
        nc.gpsimd.memset(tab_bytes[:].bitcast(I32), 0)
        nc.sync.dma_start(offsets[:], offs)
        for q in range(4):
            nc.scalar.dma_start(
                out=tab_bytes[32 * q : 32 * q + 4, :].bitcast(I32),
                in_=tab_scales[0, 4 * q : 4 * q + 4, :].bitcast(I32),
            )
        nc.sync.dma_start(out=tab_w[:], in_=tab_words[0].rearrange("p n t -> p (n t)").bitcast(I32))

        def load_rows(name, src, width):
            raw = sb.tile([P, PACK, width], F32, name=name + "_raw")
            nc.sync.dma_start(out=raw[:], in_=src.rearrange("(p t) c -> p t c", t=PACK))
            return raw

        w2_raw = load_rows("w2", w2, R)
        w1_raw = load_rows("w1", w1, R)
        x_rows = xrows.rearrange("(p m) n -> p m n", m=PACK)

        def load_x(m):
            xm = sb.tile([P, T], F32, name="x_all%d" % m, tag="x_all%d" % m, align_bytes=64)
            nc.sync.dma_start(out=xm[:], in_=x_rows[:, m, :])
            return xm

        x_rows = xrows.rearrange("(p m) n -> p m n", m=PACK)

        def load_x(m):
            xm = sb.tile([P, T], F32, name="x_all%d" % m, tag="x_all%d" % m, align_bytes=64)
            nc.sync.dma_start(out=xm[:], in_=x_rows[:, m, :])
            return xm

        wo_raw = load_rows("wo", wo, R)
        dy_raw = load_rows("dy", dy, G)
        js_col = sb.tile([P, PACK], F32, name="js_col")
        nc.sync.dma_start(out=js_col[:], in_=js.rearrange("o (p t) -> p (o t)", t=PACK))
        x_all = {m: load_x(m) for m in (0, 2, 1, 3)}
        old_sb = load_rows("old", old, R)

        ident = sb.tile([P, P], F32, name="ident")
        make_identity(nc, ident[:])

        def quantize(name, grouped, width, codes=None):
            if codes is None:
                codes = sb.tile([P, width], U32, name=name + "_codes", align_bytes=64)[:]
            scales = sb.tile([P, width], U8, name=name + "_scales", align_bytes=64)
            nc.vector.quantize_mx(
                out=codes.bitcast(FP8X4), scales=scales[:], in_=grouped.rearrange("p c t -> p (c t)")
            )
            return codes, scales[:]

        def interleave(copy, grouped, raw):
            copy(out=grouped, in_=raw[:].rearrange("p t c -> p c t"))
            return grouped

        def product(acc, lhs, rhs):
            nc.tensor.matmul_mx(
                out=acc,
                lhsT=lhs[0].bitcast(FP8X4),
                lhsT_scale=lhs[1],
                rhs=rhs[0].bitcast(FP8X4),
                rhs_scale=rhs[1],
                start=True,
                stop=True,
            )

        def turn(name, values, bank):
            pairs = values[:].bitcast(F32)
            turned = ps.tile([P, 2, P], F32, name=name + "_turned", tag=bank)
            for u in range(2):
                nc.tensor.transpose(turned[:, u, :], pairs[:, u : J // 2 : 2], ident[:])
            return turned

        def lay_out(grouped, turned):
            nc.scalar.copy(
                out=grouped.rearrange("p c t -> p (c t)").bitcast(F32).rearrange("p (c u) -> p c u", u=2),
                in_=turned[:].rearrange("p u c -> p c u"),
            )

        def pick_on_vector(m, tag):
            picked = sb.tile([P, J], BF16, name="x_picked%d" % m, tag=tag, align_bytes=64)
            nc.vector.tensor_copy(picked[:], x_all[m][:].indirect(offsets[:]))
            return picked

        def pick_on_scalar(m):
            rounded = sb.tile([P, T], BF16, name="x_rounded%d" % m, tag="shifted", align_bytes=64)
            nc.scalar.activation(out=rounded[:], in_=x_all[m][:], func=ACT.Copy)
            picked = sb.tile([P, J], BF16, name="x_picked%d" % m, align_bytes=64)
            nc.scalar.activation(picked[:], rounded[:].indirect(offsets[:]), ACT.Copy)
            return picked

        def codes_tile(name, width, tag):
            return sb.tile([P, width], U32, name=name, tag=tag, align_bytes=64)[:]

        HJ, HG = J // 2, G // 2
        listed_w = sb.tile([P, J], U32, name="listed_w", align_bytes=64)
        nc.vector.tensor_copy(listed_w[:], tab_w[:].bitcast(U32).indirect(offsets[:]))
        w2_grouped = sb.tile([P, R, PACK], BF16, name="w2_grouped", tag="w2_grouped", align_bytes=64)
        w1_grouped = sb.tile([P, R, PACK], BF16, name="w1_grouped", align_bytes=64)
        interleave(nc.scalar.copy, w2_grouped[:], w2_raw)
        interleave(nc.scalar.copy, w1_grouped[:], w1_raw)
        wo_grouped = sb.tile([P, R, PACK], BF16, name="wo_grouped", align_bytes=64)
        dy_grouped = sb.tile([P, G, PACK], BF16, name="dy_grouped", align_bytes=64)
        interleave(nc.scalar.copy, wo_grouped[:], wo_raw)
        interleave(nc.scalar.copy, dy_grouped[:], dy_raw)
        b_ps, listed = [], []
        for c in range(2):
            cols = slice(c * HJ, (c + 1) * HJ)
            listed_bytes = sb.tile(
                [P, HJ], U8, name="listed_bytes%d" % c, tag=("listed_bytes", "w2_grouped")[c], align_bytes=64
            )
            nc.vector.tensor_copy(
                listed_bytes[:], tab_bytes[:].indirect(offsets[:, c * HJ // 16 : (c + 1) * HJ // 16])
            )
            listed.append((listed_w[:, cols], listed_bytes[:]))
            if c == 0:
                w2_q = quantize("w2", w2_grouped[:], R)
            b_ps.append(ps.tile([P, HJ], F32, name="b_ps%d" % c, tag="bank_b%d" % c))
            product(b_ps[c][:], w2_q, listed[c])
        w1_q = quantize("w1", w1_grouped[:], R)
        a_ps = ps.tile([P, J], F32, name="a_ps", tag="bank_a")
        for c in range(2):
            product(a_ps[:, c * HJ : (c + 1) * HJ], w1_q, listed[c])

        def by_group(ap):
            return ap.rearrange("p (g i) -> p g i", i=8)

        def over_group(ap, groups):
            return ap.unsqueeze(2).to_broadcast([P, groups, 8])

        neg_max = sb.tile([P, G], F32, name="neg_max", tag="neg_max", align_bytes=64)
        shifted = sb.tile([P, J], F32, name="shifted", tag="shifted", align_bytes=64)
        p = sb.tile([P, J], F32, name="p")
        for c in range(2):
            nc.vector.tensor_reduce(
                out=neg_max[:, c * HG : (c + 1) * HG], in_=by_group(b_ps[c][:]), axis=AXIS.X, op=ALU.max, negate=True
            )
        for c in range(2):
            cols = slice(c * HJ, (c + 1) * HJ)
            nc.vector.tensor_tensor(
                out=by_group(shifted[:, cols]),
                in0=by_group(b_ps[c][:]),
                in1=over_group(neg_max[:, c * HG : (c + 1) * HG], HG),
                op=ALU.add,
            )
            nc.scalar.activation(out=p[:, cols], in_=shifted[:, cols], func=ACT.Exp)
        c0_codes = codes_tile("c0_codes", R + G, "neg_max")
        wo_q = quantize("wo", wo_grouped[:], R, c0_codes[:, 0:R])
        dy_q = quantize("dy", dy_grouped[:], G, c0_codes[:, R : R + G])
        c0_ps = ps.tile([P, G], F32, name="c0_ps", tag="bank_c0")
        product(c0_ps[:], wo_q, dy_q)
        js_rows = ps.tile([P, PACK, P], F32, name="js_rows", tag="bank_b0")
        for t in range(PACK):
            nc.tensor.transpose(js_rows[:, t, :], js_col[:, t : t + 1].to_broadcast([P, P]), ident[:])
        x0_turned = turn("x0", pick_on_scalar(0), "bank_x0")

        def group_sums(name, values):
            total = sb.tile([P, G], F32, name=name)
            nc.vector.tensor_reduce(out=total[:], in_=by_group(values[:]), axis=AXIS.X, op=ALU.add)
            return total

        z = group_sums("z", p)
        pa = sb.tile([P, J], F32, name="pa")
        nc.vector.tensor_tensor(out=pa[:], in0=a_ps[:], in1=p[:], op=ALU.mult)
        inv_z = sb.tile([P, G], F32, name="inv_z")
        nc.vector.reciprocal(out=inv_z[:], in_=z[:])
        n1 = group_sums("n1", pa)
        c0_by_z = sb.tile([P, G], F32, name="c0_by_z")
        nc.vector.tensor_tensor(out=c0_by_z[:], in0=c0_ps[:], in1=inv_z[:], op=ALU.mult)
        neg_mean = sb.tile([P, G], F32, name="neg_mean")
        nc.vector.scalar_tensor_tensor(
            out=neg_mean[:], in0=n1[:], scalar=-1.0, in1=inv_z[:], op0=ALU.mult, op1=ALU.mult
        )
        u1 = sb.tile([P, G], F32, name="u1", tag="shifted", align_bytes=64)
        nc.scalar.activation(out=u1[:], in_=neg_mean[:], func=ACT.Tanh)
        u1_sq = sb.tile([P, G], F32, name="u1_sq")
        nc.scalar.activation(out=u1_sq[:], in_=u1[:], func=ACT.Square)
        x2_picked = pick_on_scalar(2)

        p_js = sb.tile([P, J], F32, name="p_js")
        nc.vector.scalar_tensor_tensor(
            out=p_js[:].rearrange("p (q t) -> p q t", t=PACK),
            in0=js_rows[:].rearrange("p t q -> p q t"),
            scalar=-1.0,
            in1=p[:].rearrange("p (q t) -> p q t", t=PACK),
            op0=ALU.mult,
            op1=ALU.mult,
        )
        centred = sb.tile([P, J], F32, name="centred")
        nc.vector.tensor_tensor(
            out=by_group(centred[:]), in0=by_group(a_ps[:]), in1=over_group(neg_mean[:], G), op=ALU.add
        )
        neg_dn1 = sb.tile([P, G], F32, name="neg_dn1", tag="neg_dn1", align_bytes=64)
        nc.vector.scalar_tensor_tensor(
            out=neg_dn1[:], in0=u1_sq[:], scalar=1.0, in1=c0_by_z[:], op0=ALU.subtract, op1=ALU.mult
        )
        spread = sb.tile([P, J], F32, name="spread")
        nc.vector.tensor_tensor(out=spread[:], in0=centred[:], in1=p_js[:], op=ALU.mult)
        gs = sb.tile([P, J], BF16, name="gs", align_bytes=64)
        nc.vector.tensor_tensor(
            out=by_group(gs[:]), in0=by_group(spread[:]), in1=over_group(neg_dn1[:], G), op=ALU.mult
        )
        gt_grouped = sb.tile([P, R, PACK], BF16, name="gt_grouped", align_bytes=64)
        lay_out(gt_grouped[:], turn("gs", gs, "bank_b1"))

        x1_turned = turn("x1", pick_on_vector(1, "neg_dn1"), "bank_a")
        x01_grouped = sb.tile([P, 2 * P, PACK], BF16, name="x01_grouped", tag="shifted", align_bytes=64)
        lay_out(x01_grouped[:, 0:P, :], x0_turned)
        lay_out(x01_grouped[:, P : 2 * P, :], x1_turned)
        x2_grouped = sb.tile([P, P, PACK], BF16, name="x2_grouped", align_bytes=64)
        x3_grouped = sb.tile([P, P, PACK], BF16, name="x3_grouped", tag="x3_grouped", align_bytes=64)
        lay_out(x2_grouped[:], turn("x2", x2_picked, "bank_c0"))
        lay_out(x3_grouped[:], turn("x3", pick_on_vector(3, "x_picked3"), "bank_b0"))

        last_codes = codes_tile("last_codes", R + 3 * P, "x_all3")
        gt_q = quantize("gt", gt_grouped[:], R, last_codes[:, 0:R])
        x01_q = quantize("x01", x01_grouped[:], 2 * P, last_codes[:, R : R + 2 * P])
        x2_q = quantize("x2", x2_grouped[:], P, last_codes[:, R + 2 * P : R + 3 * P])
        x3_q = quantize("x3", x3_grouped[:], P)
        x_q = [[plane[:, 0:P] for plane in x01_q], [plane[:, P : 2 * P] for plane in x01_q], x2_q, x3_q]

        out_rows = out.rearrange("(p m) r -> p m r", m=PACK)
        result = sb.tile([P, PACK, R], F32, name="result", tag="x3_grouped", align_bytes=64)
        for c in range(2):
            tiles = slice(2 * c, 2 * c + 2)
            gw_ps = ps.tile([P, 2, R], F32, name="gw_ps%d" % c)
            for m in range(2):
                product(gw_ps[:, m, :], x_q[2 * c + m], gt_q)
            nc.vector.tensor_tensor(out=result[:, tiles, :], in0=gw_ps[:], in1=old_sb[:, tiles, :], op=ALU.add)
            nc.sync.dma_start(out=out_rows[:, tiles, :], in_=result[:, tiles, :])
